import numpy as np
import ml_dtypes


def mxq(x, axis, fmt="e4m3"):
    dtype, down = {"e4m3": (ml_dtypes.float8_e4m3fn, 7), "e5m2": (ml_dtypes.float8_e5m2, 14)}[fmt]
    v = np.moveaxis(np.asarray(x, np.float32).astype(ml_dtypes.bfloat16).astype(np.float64), axis, -1)
    blocks = v.reshape(v.shape[:-1] + (-1, 32))
    amax = np.abs(blocks).max(-1, keepdims=True)
    byte = np.maximum(np.where(amax > 0, np.frexp(amax)[1] - 1 + 127, 0) - down, 1)
    scale = np.exp2(byte - 127.0)
    codes = (blocks / scale).astype(np.float32).astype(dtype).astype(np.float64)
    return np.moveaxis((codes * scale).reshape(v.shape), -1, axis)


WIDE = False


def mx_kscale(k):
    if not WIDE:
        return np.ones(k)
    levels = np.array([10, -10, 5, -5, 0])
    if k % 512:
        return np.exp2(np.random.permutation(np.resize(levels, k // 32))).repeat(32)
    a = np.empty((k // 512, 16))
    for p in range(k // 512):
        a[p, :8] = np.random.permutation(np.resize(levels, 8))
        for g in range(8):
            far = levels[np.abs(levels - a[p, g]) >= 10]
            a[p, g + 8] = far[np.random.randint(len(far))]
    return np.exp2(a.ravel()).repeat(32)


def f64(x):
    return np.asarray(x).astype(np.float64)


def striped8(idx):
    return np.asarray(idx).reshape(8, -1, 16).transpose(0, 2, 1).reshape(128, -1).astype(np.uint16)


def unstriped8(offs):
    return offs.reshape(8, 16, -1).transpose(0, 2, 1).reshape(8, -1).astype(np.int64)


def pick8(x, idx, run):
    r = np.arange(len(x))
    return x[r[:, None], idx[r % (8 * run) // run]]


E2M1 = np.array([0.0, 0.5, 1.0, 1.5, 2.0, 3.0, 4.0, 6.0, -0.0, -0.5, -1.0, -1.5, -2.0, -3.0, -4.0, -6.0])


def pack_weight(w, fmt):
    k, n = w.shape
    w = f64(np.asarray(w, np.float32).astype(ml_dtypes.bfloat16)).reshape(k // 32, 32, n)
    amax = np.abs(w).max(1)
    if fmt == "e4m3":
        byte = np.frexp(amax)[1] - 1 + 127 - 7
    else:
        mant, ex = np.frexp(amax / 6.0)
        byte = np.where(mant > 0.5, ex, ex - 1) + 127
    byte = np.clip(np.where(amax > 0, byte, 1), 1, 254)
    scaled = (w * np.exp2(127.0 - byte)[:, None, :]).reshape(k, n).astype(np.float32)
    by_word = np.ascontiguousarray(scaled.reshape(k // 512, 128, 4, n).transpose(0, 1, 3, 2))
    if fmt == "e4m3":
        words = by_word.astype(ml_dtypes.float8_e4m3fn).view(np.uint8)
    else:
        c = by_word.astype(ml_dtypes.float4_e2m1fn).view(np.uint8) & 0xF
        words = (c[..., 0::2] | (c[..., 1::2] << 4)).reshape(k // 512, 128, 2 * n)
    return np.ascontiguousarray(words), np.ascontiguousarray(byte.astype(np.uint8).reshape(k // 512, 16, n))


def unpack_weight(words, scales, fmt):
    g, _, n = scales.shape
    words = np.ascontiguousarray(words).reshape(g, 128, n, -1)
    if fmt == "e4m3":
        vals = words.view(ml_dtypes.float8_e4m3fn).astype(np.float64)
    else:
        nib = np.empty((g, 128, n, 4), np.uint8)
        nib[..., 0::2] = words & 0xF
        nib[..., 1::2] = words >> 4
        vals = E2M1[nib]
    vals = vals * np.repeat(np.exp2(scales.astype(np.float64) - 127.0), 8, axis=1)[..., None]
    return vals.transpose(0, 1, 3, 2).reshape(g * 512, n)


D, T, I, Q = 512, 1024, 512, 128


def setup_inputs():
    n = np.random.standard_normal
    idx = np.stack([np.random.permutation(T)[:I] for _ in range(8)])
    idx2 = np.stack([np.random.permutation(T)[:I] for _ in range(8)])
    idx3 = np.stack([np.random.permutation(T)[:I] for _ in range(8)])
    idx4 = np.stack([np.random.permutation(T)[:I] for _ in range(8)])
    fd = mx_kscale(D)
    keysp = pack_weight(n((D, T)) / fd[:, None], "e4m3")
    return {
        "query": (n((D, Q)) * 0.9 / np.sqrt(D) * fd[:, None]).astype(np.float32),
        "keys_words": keysp[0],
        "keys_scales": keysp[1],
        "lam": (np.random.uniform(0.7, 1.3, (Q, 1))).astype(np.float32),
        "old": (1.0 * n((Q, T))).astype(np.float32),
        "offs": striped8(idx),
        "offs2": striped8(idx2),
        "offs3": striped8(idx3),
        "offs4": striped8(idx4),
    }


def reference(query, keys_words, keys_scales, lam, old, offs, offs2, offs3, offs4):
    idx = unstriped8(offs)
    idx2 = unstriped8(offs2)
    idx3 = unstriped8(offs3)
    idx4 = unstriped8(offs4)
    keysu = unpack_weight(keys_words, keys_scales, "e4m3")
    queryq = mxq(f64(query), 0, "e4m3")
    a = queryq.T @ keysu
    w = pick8(a, idx, 16) * f64(lam) - np.abs(pick8(a, idx2, 16) - pick8(a, idx3, 16))
    f1 = np.zeros((Q, T))
    f1[np.arange(Q)[:, None], idx4[np.arange(Q) % 128 // 16]] = w
    y = np.maximum(f1, f64(old)) + f64(old) * 0.25
    return y

@@ -1,0 +1,123 @@
+import concourse.mybir as mybir
+
+F32 = mybir.dt.float32
+BF16 = mybir.dt.bfloat16
+I32 = mybir.dt.int32
+U32 = mybir.dt.uint32
+U16 = mybir.dt.uint16
+U8 = mybir.dt.uint8
+FP8X4 = mybir.dt.float8_e4m3fn_x4
+ALU = mybir.AluOpType
+COPY = mybir.ActivationFunctionType.Copy
+
+P = 128
+PACK = 4
+D, T, SLOTS, Q = 512, 1024, 512, 128
+HALF = SLOTS // 2
+LIST_COLS = SLOTS // 16
+N_TILE = 256
+OUT_TILE = 256
+
+FLOPS = 2 * D * T * Q
+
+
+def tile_attend_betweentwo_lean_largerput_heads_kernel(
+    tc, query, keys_words, keys_scales, lam, old, offs, offs2, offs3, offs4, out
+):
+    nc = tc.nc
+    with (
+        tc.tile_pool(name="held", bufs=1) as held,
+        tc.psum_pool(name="psum", bufs=1) as psum,
+    ):
+        key_scales = held.tile([P, T], U8, name="key_scales", align_bytes=64)
+        nc.vector.memset(key_scales[:].bitcast(I32), 0)
+
+        query_raw = held.tile([P, PACK, Q], F32, name="query_raw", tag="staged")
+        nc.sync.dma_start(query_raw[:], query.rearrange("(p r) q -> p r q", r=PACK))
+        key_words = held.tile([P, T], U32, name="key_words", align_bytes=64)
+        nc.sync.dma_start(key_words[:].bitcast(I32), keys_words[0].rearrange("p c r -> p (c r)").bitcast(I32))
+        scale_rows = keys_scales[0].bitcast(I32)
+        for quad in range(4):
+            nc.sync.dma_start(key_scales[32 * quad : 32 * quad + 4, :].bitcast(I32), scale_rows[4 * quad : 4 * quad + 4, :])
+
+        list1 = held.tile([P, LIST_COLS], U16, name="list1")
+        list2 = held.tile([P, LIST_COLS], U16, name="list2")
+        list3 = held.tile([P, LIST_COLS], U16, name="list3")
+        list4 = held.tile([P, LIST_COLS], U16, name="list4")
+        nc.sync.dma_start(list3[:], offs3)
+        nc.sync.dma_start(list2[:], offs2)
+        nc.sync.dma_start(list1[:], offs)
+        nc.sync.dma_start(list4[:], offs4)
+        lam_col = held.tile([P, 1], F32, name="lam_col")
+        nc.gpsimd.dma_start(lam_col[:], lam)
+
+        placed = held.tile([P, T], F32, name="placed")
+        nc.vector.memset(placed[:], 0.0)
+
+        query_bf = held.tile([P, Q, PACK], BF16, name="query_bf", align_bytes=64)
+        nc.vector.tensor_copy(
+            query_bf[:].rearrange("p (c i) r -> p c r i", i=4), query_raw[:].rearrange("p r (c i) -> p c r i", i=4)
+        )
+        query_words = held.tile([P, Q], U32, name="query_words", align_bytes=64)
+        query_scales = held.tile([P, Q], U8, name="query_scales", align_bytes=64)
+        nc.vector.quantize_mx(query_words[:].bitcast(FP8X4), query_scales[:], query_bf[:].rearrange("p q r -> p (q r)"))
+
+        old_sb = held.tile([P, T], F32, name="old_sb", tag="staged")
+        nc.sync.dma_start(old_sb[:], old)
+
+        scores = held.tile([P, T], F32, name="scores")
+        for n in range(T // N_TILE):
+            cols = slice(n * N_TILE, (n + 1) * N_TILE)
+            bank = psum.tile([P, N_TILE], F32, name=f"bank{n}")
+            nc.tensor.matmul_mx(
+                bank[:],
+                lhsT=query_words[:].bitcast(FP8X4),
+                lhsT_scale=query_scales[:],
+                rhs=key_words[:, cols].bitcast(FP8X4),
+                rhs_scale=key_scales[:, cols],
+                start=True,
+                stop=True,
+            )
+            if n % 2 == 0:
+                nc.scalar.activation(scores[:, cols], bank[:], COPY)
+            else:
+                nc.vector.tensor_copy(scores[:, cols], bank[:])
+
+        first, second = slice(0, HALF), slice(HALF, SLOTS)
+
+        def listed(window, offsets, slots):
+            return window[:].indirect(offsets[:, slots.start // 16 : slots.stop // 16])
+
+        picked1 = held.tile([P, SLOTS], F32, name="picked1")
+        picked2 = held.tile([P, HALF], F32, name="picked2")
+        picked3 = held.tile([P, SLOTS], F32, name="picked3")
+        scaled1 = held.tile([P, SLOTS], F32, name="scaled1")
+        diff = held.tile([P, SLOTS], F32, name="diff")
+        neg_abs = held.tile([P, SLOTS], F32, name="neg_abs")
+
+        for slots in (first, second):
+            nc.scalar.activation(picked3[:, slots], listed(scores, list3, slots), COPY)
+        nc.vector.tensor_copy(picked2[:], listed(scores, list2, second))
+        nc.vector.tensor_tensor(diff[:, first], listed(scores, list2, first), picked3[:, first], ALU.subtract)
+        nc.vector.tensor_tensor(diff[:, second], picked2[:], picked3[:, second], ALU.subtract)
+        nc.vector.scalar_tensor_tensor(neg_abs[:], diff[:], -1.0, diff[:], ALU.mult, ALU.min)
+        for slots in (first, second):
+            nc.scalar.activation(picked1[:, slots], listed(scores, list1, slots), COPY)
+            nc.scalar.activation(scaled1[:, slots], picked1[:, slots], COPY, scale=lam_col[:])
+            nc.vector.tensor_tensor(listed(placed, list4, slots), scaled1[:, slots], neg_abs[:, slots], ALU.add)
+
+        larger = held.tile([P, T], F32, name="larger")
+        result = held.tile([P, T], F32, name="result")
+        pieces = [slice(c, c + OUT_TILE) for c in range(0, T, OUT_TILE)]
+
+        def finish(n):
+            cols = pieces[n]
+            nc.vector.scalar_tensor_tensor(result[:, cols], old_sb[:, cols], 0.25, larger[:, cols], ALU.mult, ALU.add)
+            queue = nc.sync if n % 2 == 0 else nc.scalar
+            queue.dma_start(out[:, cols], result[:, cols])
+
+        for n, cols in enumerate(pieces):
+            nc.vector.tensor_tensor(larger[:, cols], placed[:, cols], old_sb[:, cols], ALU.max)
+            if n > 0:
+                finish(n - 1)
+        finish(len(pieces) - 1)

@@ -30,15 +30,18 @@ def tile_attend_betweentwo_lean_largerput_heads_kernel(
         tc.psum_pool(name="psum", bufs=1) as psum,
     ):
         key_scales = held.tile([P, T], U8, name="key_scales", align_bytes=64)
-        nc.vector.memset(key_scales[:].bitcast(I32), 0)
 
         query_raw = held.tile([P, PACK, Q], F32, name="query_raw", tag="staged")
         nc.sync.dma_start(query_raw[:], query.rearrange("(p r) q -> p r q", r=PACK))
-        key_words = held.tile([P, T], U32, name="key_words", align_bytes=64)
-        nc.sync.dma_start(key_words[:].bitcast(I32), keys_words[0].rearrange("p c r -> p (c r)").bitcast(I32))
         scale_rows = keys_scales[0].bitcast(I32)
         for quad in range(4):
             nc.sync.dma_start(key_scales[32 * quad : 32 * quad + 4, :].bitcast(I32), scale_rows[4 * quad : 4 * quad + 4, :])
+        words_in = keys_words[0].rearrange("p c r -> p (c r)").bitcast(I32)
+        key_words = []
+        for n in range(2):
+            part = held.tile([P, T // 2], U32, name=f"key_words{n}", align_bytes=64)
+            nc.sync.dma_start(part[:].bitcast(I32), words_in[:, n * T // 2 : (n + 1) * T // 2])
+            key_words.append(part)
 
         list1 = held.tile([P, LIST_COLS], U16, name="list1")
         list2 = held.tile([P, LIST_COLS], U16, name="list2")
@@ -49,7 +52,7 @@ def tile_attend_betweentwo_lean_largerput_heads_kernel(
         nc.sync.dma_start(list1[:], offs)
         nc.sync.dma_start(list4[:], offs4)
         lam_col = held.tile([P, 1], F32, name="lam_col")
-        nc.gpsimd.dma_start(lam_col[:], lam)
+        nc.sync.dma_start(lam_col[:], lam)
 
         placed = held.tile([P, T], F32, name="placed")
         nc.vector.memset(placed[:], 0.0)
@@ -73,7 +76,7 @@ def tile_attend_betweentwo_lean_largerput_heads_kernel(
                 bank[:],
                 lhsT=query_words[:].bitcast(FP8X4),
                 lhsT_scale=query_scales[:],
-                rhs=key_words[:, cols].bitcast(FP8X4),
+                rhs=key_words[n // 2][:, n % 2 * N_TILE : (n % 2 + 1) * N_TILE].bitcast(FP8X4),
                 rhs_scale=key_scales[:, cols],
                 start=True,
                 stop=True,

@@ -9,14 +9,15 @@ U8 = mybir.dt.uint8
 FP8X4 = mybir.dt.float8_e4m3fn_x4
 ALU = mybir.AluOpType
 COPY = mybir.ActivationFunctionType.Copy
+ABS = mybir.ActivationFunctionType.Abs
 
 P = 128
 PACK = 4
 D, T, SLOTS, Q = 512, 1024, 512, 128
 HALF = SLOTS // 2
 LIST_COLS = SLOTS // 16
-N_TILE = 256
-OUT_TILE = 256
+SCORE_WIDTHS = (512, 256, 128, 128)
+OUT_EDGES = (0, 320, 640, 896, 1024)
 
 FLOPS = 2 * D * T * Q
 
@@ -47,8 +48,8 @@ def tile_attend_betweentwo_lean_largerput_heads_kernel(
         list2 = held.tile([P, LIST_COLS], U16, name="list2")
         list3 = held.tile([P, LIST_COLS], U16, name="list3")
         list4 = held.tile([P, LIST_COLS], U16, name="list4")
-        nc.sync.dma_start(list3[:], offs3)
         nc.sync.dma_start(list2[:], offs2)
+        nc.sync.dma_start(list3[:], offs3)
         nc.sync.dma_start(list1[:], offs)
         nc.sync.dma_start(list4[:], offs4)
         lam_col = held.tile([P, 1], F32, name="lam_col")
@@ -69,22 +70,25 @@ def tile_attend_betweentwo_lean_largerput_heads_kernel(
         nc.sync.dma_start(old_sb[:], old)
 
         scores = held.tile([P, T], F32, name="scores")
-        for n in range(T // N_TILE):
-            cols = slice(n * N_TILE, (n + 1) * N_TILE)
-            bank = psum.tile([P, N_TILE], F32, name=f"bank{n}")
+        start = 0
+        for n, width in enumerate(SCORE_WIDTHS):
+            cols = slice(start, start + width)
+            words = key_words[start // (T // 2)][:, start % (T // 2) : start % (T // 2) + width]
+            bank = psum.tile([P, width], F32, name=f"bank{n}")
             nc.tensor.matmul_mx(
                 bank[:],
                 lhsT=query_words[:].bitcast(FP8X4),
                 lhsT_scale=query_scales[:],
-                rhs=key_words[n // 2][:, n % 2 * N_TILE : (n % 2 + 1) * N_TILE].bitcast(FP8X4),
+                rhs=words.bitcast(FP8X4),
                 rhs_scale=key_scales[:, cols],
                 start=True,
                 stop=True,
             )
-            if n % 2 == 0:
+            if n in (0, len(SCORE_WIDTHS) - 1):
                 nc.scalar.activation(scores[:, cols], bank[:], COPY)
             else:
                 nc.vector.tensor_copy(scores[:, cols], bank[:])
+            start = start + width
 
         first, second = slice(0, HALF), slice(HALF, SLOTS)
 
@@ -92,26 +96,35 @@ def tile_attend_betweentwo_lean_largerput_heads_kernel(
             return window[:].indirect(offsets[:, slots.start // 16 : slots.stop // 16])
 
         picked1 = held.tile([P, SLOTS], F32, name="picked1")
-        picked2 = held.tile([P, HALF], F32, name="picked2")
+        picked2 = held.tile([P, SLOTS], F32, name="picked2")
         picked3 = held.tile([P, SLOTS], F32, name="picked3")
         scaled1 = held.tile([P, SLOTS], F32, name="scaled1")
         diff = held.tile([P, SLOTS], F32, name="diff")
+        distance = held.tile([P, HALF], F32, name="distance")
         neg_abs = held.tile([P, SLOTS], F32, name="neg_abs")
 
         for slots in (first, second):
-            nc.scalar.activation(picked3[:, slots], listed(scores, list3, slots), COPY)
-        nc.vector.tensor_copy(picked2[:], listed(scores, list2, second))
-        nc.vector.tensor_tensor(diff[:, first], listed(scores, list2, first), picked3[:, first], ALU.subtract)
-        nc.vector.tensor_tensor(diff[:, second], picked2[:], picked3[:, second], ALU.subtract)
-        nc.vector.scalar_tensor_tensor(neg_abs[:], diff[:], -1.0, diff[:], ALU.mult, ALU.min)
+            nc.vector.tensor_copy(picked2[:, slots], listed(scores, list2, slots))
+        nc.scalar.activation(picked3[:, first], listed(scores, list3, first), COPY)
+        nc.scalar.activation(picked1[:, first], listed(scores, list1, first), COPY)
+        nc.scalar.activation(picked3[:, second], listed(scores, list3, second), COPY)
+        nc.scalar.activation(picked1[:, second], listed(scores, list1, second), COPY)
+
+        nc.vector.tensor_tensor(diff[:, first], picked2[:, first], picked3[:, first], ALU.subtract)
+        nc.vector.scalar_tensor_tensor(neg_abs[:, first], diff[:, first], -1.0, diff[:, first], ALU.mult, ALU.min)
+        nc.vector.tensor_scalar_mul(scaled1[:, first], picked1[:, first], lam_col[:])
+        nc.vector.tensor_tensor(diff[:, second], picked2[:, second], picked3[:, second], ALU.subtract)
+
+        nc.scalar.activation(distance[:], diff[:, second], ABS)
+        nc.scalar.activation(scaled1[:, second], picked1[:, second], COPY, scale=lam_col[:])
+        nc.scalar.activation(neg_abs[:, second], distance[:], COPY, scale=-1.0)
+
         for slots in (first, second):
-            nc.scalar.activation(picked1[:, slots], listed(scores, list1, slots), COPY)
-            nc.scalar.activation(scaled1[:, slots], picked1[:, slots], COPY, scale=lam_col[:])
             nc.vector.tensor_tensor(listed(placed, list4, slots), scaled1[:, slots], neg_abs[:, slots], ALU.add)
 
         larger = held.tile([P, T], F32, name="larger")
         result = held.tile([P, T], F32, name="result")
-        pieces = [slice(c, c + OUT_TILE) for c in range(0, T, OUT_TILE)]
+        pieces = [slice(lo, hi) for lo, hi in zip(OUT_EDGES, OUT_EDGES[1:])]
 
         def finish(n):
             cols = pieces[n]

import concourse.mybir as mybir

F32 = mybir.dt.float32
BF16 = mybir.dt.bfloat16
I32 = mybir.dt.int32
U32 = mybir.dt.uint32
U16 = mybir.dt.uint16
U8 = mybir.dt.uint8
FP8X4 = mybir.dt.float8_e4m3fn_x4
ALU = mybir.AluOpType
COPY = mybir.ActivationFunctionType.Copy
ABS = mybir.ActivationFunctionType.Abs

P = 128
PACK = 4
D, T, SLOTS, Q = 512, 1024, 512, 128
HALF = SLOTS // 2
LIST_COLS = SLOTS // 16
SCORE_WIDTHS = (512, 256, 128, 128)
OUT_EDGES = (0, 320, 640, 896, 1024)

FLOPS = 2 * D * T * Q


def tile_attend_betweentwo_lean_largerput_heads_kernel(
    tc, query, keys_words, keys_scales, lam, old, offs, offs2, offs3, offs4, out
):
    nc = tc.nc
    with (
        tc.tile_pool(name="held", bufs=1) as held,
        tc.psum_pool(name="psum", bufs=1) as psum,
    ):
        key_scales = held.tile([P, T], U8, name="key_scales", align_bytes=64)

        query_raw = held.tile([P, PACK, Q], F32, name="query_raw", tag="staged")
        nc.sync.dma_start(query_raw[:], query.rearrange("(p r) q -> p r q", r=PACK))
        scale_rows = keys_scales[0].bitcast(I32)
        for quad in range(4):
            nc.sync.dma_start(key_scales[32 * quad : 32 * quad + 4, :].bitcast(I32), scale_rows[4 * quad : 4 * quad + 4, :])
        words_in = keys_words[0].rearrange("p c r -> p (c r)").bitcast(I32)
        key_words = []
        for n in range(2):
            part = held.tile([P, T // 2], U32, name=f"key_words{n}", align_bytes=64)
            nc.sync.dma_start(part[:].bitcast(I32), words_in[:, n * T // 2 : (n + 1) * T // 2])
            key_words.append(part)

        list1 = held.tile([P, LIST_COLS], U16, name="list1")
        list2 = held.tile([P, LIST_COLS], U16, name="list2")
        list3 = held.tile([P, LIST_COLS], U16, name="list3")
        list4 = held.tile([P, LIST_COLS], U16, name="list4")
        nc.sync.dma_start(list2[:], offs2)
        nc.sync.dma_start(list3[:], offs3)
        nc.sync.dma_start(list1[:], offs)
        nc.sync.dma_start(list4[:], offs4)
        lam_col = held.tile([P, 1], F32, name="lam_col")
        nc.sync.dma_start(lam_col[:], lam)

        placed = held.tile([P, T], F32, name="placed")
        nc.vector.memset(placed[:], 0.0)

        query_bf = held.tile([P, Q, PACK], BF16, name="query_bf", align_bytes=64)
        nc.vector.tensor_copy(
            query_bf[:].rearrange("p (c i) r -> p c r i", i=4), query_raw[:].rearrange("p r (c i) -> p c r i", i=4)
        )
        query_words = held.tile([P, Q], U32, name="query_words", align_bytes=64)
        query_scales = held.tile([P, Q], U8, name="query_scales", align_bytes=64)
        nc.vector.quantize_mx(query_words[:].bitcast(FP8X4), query_scales[:], query_bf[:].rearrange("p q r -> p (q r)"))

        old_sb = held.tile([P, T], F32, name="old_sb", tag="staged")
        nc.sync.dma_start(old_sb[:], old)

        scores = held.tile([P, T], F32, name="scores")
        start = 0
        for n, width in enumerate(SCORE_WIDTHS):
            cols = slice(start, start + width)
            words = key_words[start // (T // 2)][:, start % (T // 2) : start % (T // 2) + width]
            bank = psum.tile([P, width], F32, name=f"bank{n}")
            nc.tensor.matmul_mx(
                bank[:],
                lhsT=query_words[:].bitcast(FP8X4),
                lhsT_scale=query_scales[:],
                rhs=words.bitcast(FP8X4),
                rhs_scale=key_scales[:, cols],
                start=True,
                stop=True,
            )
            if n in (0, len(SCORE_WIDTHS) - 1):
                nc.scalar.activation(scores[:, cols], bank[:], COPY)
            else:
                nc.vector.tensor_copy(scores[:, cols], bank[:])
            start = start + width

        first, second = slice(0, HALF), slice(HALF, SLOTS)

        def listed(window, offsets, slots):
            return window[:].indirect(offsets[:, slots.start // 16 : slots.stop // 16])

        picked1 = held.tile([P, SLOTS], F32, name="picked1")
        picked2 = held.tile([P, SLOTS], F32, name="picked2")
        picked3 = held.tile([P, SLOTS], F32, name="picked3")
        scaled1 = held.tile([P, SLOTS], F32, name="scaled1")
        diff = held.tile([P, SLOTS], F32, name="diff")
        distance = held.tile([P, HALF], F32, name="distance")
        neg_abs = held.tile([P, SLOTS], F32, name="neg_abs")

        for slots in (first, second):
            nc.vector.tensor_copy(picked2[:, slots], listed(scores, list2, slots))
        nc.scalar.activation(picked3[:, first], listed(scores, list3, first), COPY)
        nc.scalar.activation(picked1[:, first], listed(scores, list1, first), COPY)
        nc.scalar.activation(picked3[:, second], listed(scores, list3, second), COPY)
        nc.scalar.activation(picked1[:, second], listed(scores, list1, second), COPY)

        nc.vector.tensor_tensor(diff[:, first], picked2[:, first], picked3[:, first], ALU.subtract)
        nc.vector.scalar_tensor_tensor(neg_abs[:, first], diff[:, first], -1.0, diff[:, first], ALU.mult, ALU.min)
        nc.vector.tensor_scalar_mul(scaled1[:, first], picked1[:, first], lam_col[:])
        nc.vector.tensor_tensor(diff[:, second], picked2[:, second], picked3[:, second], ALU.subtract)

        nc.scalar.activation(distance[:], diff[:, second], ABS)
        nc.scalar.activation(scaled1[:, second], picked1[:, second], COPY, scale=lam_col[:])
        nc.scalar.activation(neg_abs[:, second], distance[:], COPY, scale=-1.0)

        for slots in (first, second):
            nc.vector.tensor_tensor(listed(placed, list4, slots), scaled1[:, slots], neg_abs[:, slots], ALU.add)

        larger = held.tile([P, T], F32, name="larger")
        result = held.tile([P, T], F32, name="result")
        pieces = [slice(lo, hi) for lo, hi in zip(OUT_EDGES, OUT_EDGES[1:])]

        def finish(n):
            cols = pieces[n]
            nc.vector.scalar_tensor_tensor(result[:, cols], old_sb[:, cols], 0.25, larger[:, cols], ALU.mult, ALU.add)
            queue = nc.sync if n % 2 == 0 else nc.scalar
            queue.dma_start(out[:, cols], result[:, cols])

        for n, cols in enumerate(pieces):
            nc.vector.tensor_tensor(larger[:, cols], placed[:, cols], old_sb[:, cols], ALU.max)
            if n > 0:
                finish(n - 1)
        finish(len(pieces) - 1)
